import numpy as np
import ml_dtypes


def mxq(x, axis, fmt="e4m3"):
    dtype, down = {"e4m3": (ml_dtypes.float8_e4m3fn, 7), "e5m2": (ml_dtypes.float8_e5m2, 14)}[fmt]
    v = np.moveaxis(np.asarray(x, np.float32).astype(ml_dtypes.bfloat16).astype(np.float64), axis, -1)
    blocks = v.reshape(v.shape[:-1] + (-1, 32))
    amax = np.abs(blocks).max(-1, keepdims=True)
    byte = np.maximum(np.where(amax > 0, np.frexp(amax)[1] - 1 + 127, 0) - down, 1)
    scale = np.exp2(byte - 127.0)
    codes = (blocks / scale).astype(np.float32).astype(dtype).astype(np.float64)
    return np.moveaxis((codes * scale).reshape(v.shape), -1, axis)


WIDE = False


def mx_kscale(k):
    if not WIDE:
        return np.ones(k)
    levels = np.array([10, -10, 5, -5, 0])
    if k % 512:
        return np.exp2(np.random.permutation(np.resize(levels, k // 32))).repeat(32)
    a = np.empty((k // 512, 16))
    for p in range(k // 512):
        a[p, :8] = np.random.permutation(np.resize(levels, 8))
        for g in range(8):
            far = levels[np.abs(levels - a[p, g]) >= 10]
            a[p, g + 8] = far[np.random.randint(len(far))]
    return np.exp2(a.ravel()).repeat(32)


def f64(x):
    return np.asarray(x).astype(np.float64)


def striped(idx):
    return np.tile(np.asarray(idx).reshape(-1, 16).T, (8, 1)).astype(np.uint16)


def unstriped(offs):
    return offs[:16].T.reshape(-1).astype(np.int64)


def bf(x):
    return np.asarray(x, np.float32).astype(ml_dtypes.bfloat16)


def planes(Y):
    r, m = Y.shape
    b = f64(bf(Y)).reshape(r // 32, 32, m)
    amax = np.abs(b).max(1)
    byte = np.clip(np.where(amax > 0, np.frexp(amax)[1] - 1 + 127 - 7, 1), 1, 254)
    codes = (b * np.exp2(127.0 - byte)[:, None, :]).reshape(r, m).astype(np.float32).astype(ml_dtypes.float8_e4m3fn).view(np.uint8)
    words = codes.reshape(r // 512, 128, 4, m).transpose(0, 1, 3, 2)
    return np.ascontiguousarray(words), np.ascontiguousarray(byte.astype(np.uint8).reshape(r // 512, 16, m))


D, T, I, Q, E = 512, 1024, 512, 256, 512


def setup_inputs():
    n = np.random.standard_normal
    idx = np.random.permutation(T)[:I]
    idx2 = np.random.permutation(T)[:I]
    fd = mx_kscale(D)
    fi = mx_kscale(I)
    return {
        "query": (n((D, Q)) * 0.25 / np.sqrt(D) * fd[:, None]).astype(np.float32),
        "keys": (n((D, T)) / fd[:, None]).astype(np.float32),
        "size": (np.random.uniform(0.5, 2.0, (1, I)) * fi).astype(np.float32),
        "vals": (n((E, T))).astype(np.float32),
        "vsc": (np.random.uniform(0.3, 1.0, (I, 1)) / fi[:, None]).astype(np.float32),
        "offs": striped(idx),
        "offs2": striped(idx2),
    }


def reference(query, keys, size, vals, vsc, offs, offs2):
    idx = unstriped(offs)
    idx2 = unstriped(offs2)
    km = np.maximum(f64(keys)[:, idx], f64(keys)[:, idx2])
    queryq = mxq(f64(query), 0, "e4m3")
    kmq = mxq(km, 0, "e4m3")
    a = queryq.T @ kmq
    p = np.exp(a - np.max(a, axis=1, keepdims=True))
    w = p * f64(size) / np.sum(p, axis=1, keepdims=True)
    wt = w.T
    v1 = f64(vals)[:, idx].T
    v2 = f64(vals)[:, idx2].T
    vv = (v1 + v2) * f64(vsc)
    vvq = mxq(vv, 0, "e4m3")
    wtq = mxq(wt, 0, "e4m3")
    o = vvq.T @ wtq
    words, scales = planes(o)
    return o, words, scales

@@ -1,0 +1,235 @@
+from contextlib import ExitStack
+
+import concourse.mybir as mybir
+from concourse.masks import make_identity
+
+D, T, I, Q, E = 512, 1024, 512, 256, 512
+FLOPS = 2 * D * Q * I + 2 * I * E * Q
+
+F32 = mybir.dt.float32
+BF16 = mybir.dt.bfloat16
+U32 = mybir.dt.uint32
+I32 = mybir.dt.int32
+U16 = mybir.dt.uint16
+U8 = mybir.dt.uint8
+FP8X4 = mybir.dt.float8_e4m3fn_x4
+ALU = mybir.AluOpType
+ACT = mybir.ActivationFunctionType
+
+P = 128
+PACK = 4
+HALVES = Q // P
+
+
+def woven(ap):
+    return ap.rearrange("p (c i) t -> p c t i", i=2)
+
+
+def planar(ap):
+    return ap.rearrange("p t (c i) -> p c t i", i=2)
+
+
+def flat(ap):
+    return ap.rearrange("p c t -> p (c t)")
+
+
+def tile_attend_maxmerge_pl_kernel(tc, query, keys, size, vals, vsc, offs, offs2, out_0, out_1, out_2):
+    nc = tc.nc
+    with ExitStack() as ctx:
+        lists = ctx.enter_context(tc.tile_pool(name="lists", bufs=1))
+        sb = ctx.enter_context(tc.tile_pool(name="sb", bufs=1))
+        ps = ctx.enter_context(tc.psum_pool(name="ps", bufs=1))
+
+        list_a = lists.tile([P, I // 16], U16, name="list_a")
+        list_b = lists.tile([P, I // 16], U16, name="list_b")
+        key_planes = keys.rearrange("(p t) n -> t p n", t=PACK)
+        val_planes = vals.rearrange("(p t) n -> t p n", t=PACK)
+        key_win = [sb.tile([P, T], F32, name="key_win%d" % t) for t in range(PACK)]
+        val_win = [sb.tile([P, T], F32, name="val_win%d" % t) for t in range(PACK)]
+        q_raw = sb.tile([P, PACK, Q], F32, name="q_raw")
+        factor_rows = sb.tile([P, P], F32, name="factor_rows")
+        ident = sb.tile([P, P], F32, name="ident")
+        warm = sb.tile([P, 2], F32, name="warm")
+
+        nc.vector.memset(factor_rows[:], 0.0)
+        nc.vector.memset(warm[:, 0:1], 0.0)
+        make_identity(nc, ident[:])
+        nc.scalar.activation(out=warm[:, 1:2], in_=warm[:, 0:1], func=ACT.Exp)
+
+        nc.sync.dma_start(list_a[:], offs)
+        nc.sync.dma_start(out=key_win[0][:], in_=key_planes[0])
+        nc.sync.dma_start(list_b[:], offs2)
+        nc.sync.dma_start(out=key_win[1][:], in_=key_planes[1])
+        nc.sync.dma_start(out=q_raw[:], in_=query.rearrange("(p t) q -> p t q", t=PACK))
+        nc.sync.dma_start(out=key_win[2][:], in_=key_planes[2])
+        nc.sync.dma_start(out=key_win[3][:], in_=key_planes[3])
+        nc.sync.dma_start(
+            out=factor_rows[0:PACK, :].rearrange("t (b j) -> t b j", j=8),
+            in_=size.rearrange("o (b t j) -> (o t) b j", t=PACK, j=8),
+        )
+        nc.sync.dma_start(
+            out=factor_rows[PACK : 2 * PACK, :].rearrange("t (b j) -> t b j", j=8),
+            in_=vsc.rearrange("(b t j) o -> t b (j o)", t=PACK, j=8),
+        )
+        for r in range(PACK):
+            nc.sync.dma_start(out=val_win[r][:], in_=val_planes[r])
+
+        q_bf = sb.tile([P, Q, PACK], BF16, name="q_bf", align_bytes=64)
+        q_codes = sb.tile([P, Q], U32, name="q_codes", align_bytes=64)
+        q_scales = sb.tile([P, Q], U8, name="q_scales", align_bytes=64)
+        nc.scalar.copy(out=woven(q_bf[:]), in_=planar(q_raw[:]))
+
+        factor_bank = ps.tile([P, P], F32, name="factor_bank")
+        nc.tensor.transpose(factor_bank[:], factor_rows[:], ident[:])
+        size_cols = sb.tile([P, PACK], F32, name="size_cols", tag="slot_2_1", align_bytes=64)
+        vsc_cols = sb.tile([P, PACK], F32, name="vsc_cols")
+        nc.scalar.copy(out=size_cols[:], in_=factor_bank[:, 0:PACK])
+        nc.scalar.copy(out=vsc_cols[:], in_=factor_bank[:, PACK : 2 * PACK])
+
+        key_a = sb.tile([P, PACK, I], F32, name="key_a")
+        key_b = sb.tile([P, PACK, I], F32, name="key_b")
+        for t in range(PACK):
+            nc.vector.tensor_copy(key_a[:, t, :], key_win[t][:].indirect(list_a[:]))
+            nc.vector.tensor_copy(key_b[:, t, :], key_win[t][:].indirect(list_b[:]))
+            if t == 2:
+                nc.vector.quantize_mx(out=q_codes[:].bitcast(FP8X4), scales=q_scales[:], in_=flat(q_bf[:]))
+        km_bf = sb.tile([P, I, PACK], BF16, name="km_bf", align_bytes=64)
+        km_codes = sb.tile([P, I], U32, name="km_codes", align_bytes=64)
+        km_scales = sb.tile([P, I], U8, name="km_scales", align_bytes=64)
+        nc.vector.tensor_tensor(out=woven(km_bf[:]), in0=planar(key_a[:]), in1=planar(key_b[:]), op=ALU.max)
+
+        def gather_vals(r, which):
+            got = sb.tile([P, I], F32, name="val_%d_%d" % (r, which), tag="slot_%d_%d" % (r, which), align_bytes=64)
+            nc.vector.tensor_copy(
+                got[:].bitcast(U32).rearrange("p (t b j) -> p b t j", t=PACK, j=8),
+                val_win[r][:].bitcast(U32).indirect((list_a, list_b)[which][:]),
+            )
+            return got
+
+        def turn(bank, got, first, last):
+            for t in range(PACK):
+                nc.tensor.matmul(
+                    out=bank[:, t, :], lhsT=got[:, t * P : (t + 1) * P], rhs=ident[:], is_transpose=True,
+                    start=(first and t == 0), stop=(last and t == PACK - 1),
+                )
+
+        def spread(col):
+            return col.unsqueeze(1).unsqueeze(3).to_broadcast([P, P // 2, PACK, 2])
+
+        vv_bf = [sb.tile([P, P, PACK], BF16, name="vv_bf%d" % r, tag=("slot_3_0", "slot_3_1", "vv_bf2", "vv_bf3")[r], align_bytes=64) for r in range(PACK)]
+        vv_codes = [sb.tile([P, P], U32, name="vv_codes%d" % r, align_bytes=64) for r in range(PACK)]
+        vv_scales = [sb.tile([P, P], U8, name="vv_scales%d" % r, align_bytes=64) for r in range(PACK)]
+        v_bank = {}
+
+        def value_step(r, which):
+            if which == 0:
+                v_bank[r] = ps.tile([P, PACK, P], F32, name="v_bank", tag="v_bank", bufs=3)
+            turn(v_bank[r], gather_vals(r, which), which == 0, which == 1)
+
+        def scale_vals(r):
+            if r == PACK - 1:
+                nc.vector.tensor_tensor(
+                    out=woven(vv_bf[r][:]), in0=planar(v_bank[r][:]), in1=spread(vsc_cols[:]), op=ALU.mult
+                )
+            else:
+                for t in range(PACK):
+                    nc.scalar.activation(
+                        out=vv_bf[r][:, :, t], in_=v_bank[r][:, t, :], func=ACT.Copy, scale=vsc_cols[:, t : t + 1]
+                    )
+
+        def quantize_vals(r):
+            nc.vector.quantize_mx(out=vv_codes[r][:].bitcast(FP8X4), scales=vv_scales[r][:], in_=flat(vv_bf[r][:]))
+
+        value_step(0, 0)
+        nc.vector.quantize_mx(out=km_codes[:].bitcast(FP8X4), scales=km_scales[:], in_=flat(km_bf[:]))
+        scores = [ps.tile([P, I], F32, name="scores", tag="scores", bufs=2) for h in range(HALVES)]
+        for h in range(HALVES):
+            nc.tensor.matmul_mx(
+                out=scores[h][:],
+                lhsT=q_codes[:, h * P : (h + 1) * P].bitcast(FP8X4), lhsT_scale=q_scales[:, h * P : (h + 1) * P],
+                rhs=km_codes[:].bitcast(FP8X4), rhs_scale=km_scales[:], start=True, stop=True,
+            )
+        value_step(0, 1)
+
+        neg_max = [sb.tile([P, 1], F32, name="neg_max%d" % h, tag=("slot_1_0", "neg_max1")[h], align_bytes=64) for h in range(HALVES)]
+        sums = sb.tile([P, HALVES], F32, name="sums", tag="slot_1_1", align_bytes=64)
+        inv = sb.tile([P, HALVES], F32, name="inv")
+        prob = [sb.tile([P, I], F32, name="prob%d" % h) for h in range(HALVES)]
+        normed = [sb.tile([P, I], F32, name="normed%d" % h) for h in range(HALVES)]
+        for h in range(HALVES):
+            nc.vector.tensor_reduce(out=neg_max[h][:], in_=scores[h][:], axis=mybir.AxisListType.X, op=ALU.max, negate=True)
+            nc.scalar.activation(
+                out=prob[h][:].rearrange("p (t b j) -> p t b j", t=PACK, j=8),
+                in_=scores[h][:].rearrange("p (b t j) -> p t b j", t=PACK, j=8),
+                func=ACT.Exp, bias=neg_max[h][:], accum_out=sums[:, h : h + 1],
+            )
+        value_step(1, 0)
+        nc.vector.reciprocal(out=inv[:], in_=sums[:])
+        w_bank = []
+        for h in range(HALVES):
+            nc.scalar.activation(out=normed[h][:], in_=prob[h][:], func=ACT.Copy, scale=inv[:, h : h + 1])
+            bank = ps.tile([P, PACK, P], F32, name="w_bank", tag="scores", bufs=2)
+            turn(bank, normed[h], True, True)
+            w_bank.append(bank)
+        scale_vals(0)
+        value_step(1, 1)
+        value_step(2, 0)
+        w_bf = sb.tile([P, Q, PACK], BF16, name="w_bf", align_bytes=64)
+        w_codes = sb.tile([P, Q], U32, name="w_codes", align_bytes=64)
+        w_scales = sb.tile([P, Q], U8, name="w_scales", align_bytes=64)
+        for h in range(HALVES):
+            nc.vector.tensor_tensor(
+                out=woven(w_bf[:, h * P : (h + 1) * P, :]), in0=planar(w_bank[h][:]), in1=spread(size_cols[:]), op=ALU.mult
+            )
+        scale_vals(1)
+        value_step(2, 1)
+        nc.vector.quantize_mx(out=w_codes[:].bitcast(FP8X4), scales=w_scales[:], in_=flat(w_bf[:]))
+        quantize_vals(0)
+        quantize_vals(1)
+        scale_vals(2)
+
+        out_bank = [ps.tile([P, PACK, P], F32, name="out_bank%d" % h) for h in range(HALVES)]
+
+        def product(r):
+            for h in range(HALVES):
+                nc.tensor.matmul_mx(
+                    out=out_bank[h][:, r, :],
+                    lhsT=vv_codes[r][:].bitcast(FP8X4), lhsT_scale=vv_scales[r][:],
+                    rhs=w_codes[:, h * P : (h + 1) * P].bitcast(FP8X4), rhs_scale=w_scales[:, h * P : (h + 1) * P],
+                    start=True, stop=True,
+                )
+
+        product(0)
+        product(1)
+        value_step(3, 0)
+        value_step(3, 1)
+        quantize_vals(2)
+        product(2)
+        out_rows = out_0.rearrange("(p r) q -> p r q", r=PACK)
+        early = sb.tile([P, PACK - 1, Q], F32, name="early")
+        late = sb.tile([P, Q], F32, name="late")
+        for h in range(HALVES):
+            nc.scalar.copy(out=early[:, :, h * P : (h + 1) * P], in_=out_bank[h][:, 0 : PACK - 1, :])
+        nc.sync.dma_start(out=out_rows[:, 0 : PACK - 1, :], in_=early[:])
+        scale_vals(3)
+        quantize_vals(3)
+        product(3)
+
+        o_bf = [sb.tile([P, P, PACK], BF16, name="o_bf%d" % h, align_bytes=64) for h in range(HALVES)]
+        o_codes = sb.tile([P, Q], U32, name="o_codes", align_bytes=64)
+        o_scales = sb.tile([P, Q], U8, name="o_scales", align_bytes=64)
+        nc.vector.tensor_copy(out=woven(o_bf[0][:]), in_=planar(out_bank[0][:]))
+        nc.scalar.copy(out=woven(o_bf[1][:]), in_=planar(out_bank[1][:]))
+        for h in range(HALVES):
+            nc.vector.quantize_mx(
+                out=o_codes[:, h * P : (h + 1) * P].bitcast(FP8X4), scales=o_scales[:, h * P : (h + 1) * P], in_=flat(o_bf[h][:])
+            )
+        for h in range(HALVES):
+            nc.scalar.copy(out=late[:, h * P : (h + 1) * P], in_=out_bank[h][:, PACK - 1, :])
+        nc.sync.dma_start(out=out_1[0].rearrange("p c r -> p (c r)").bitcast(I32), in_=o_codes[:].bitcast(I32))
+        for quad in range(4):
+            queue = nc.sync if quad % 2 == 0 else nc.scalar
+            queue.dma_start(
+                out=out_2[0, 4 * quad : 4 * quad + 4, :].bitcast(I32), in_=o_scales[32 * quad : 32 * quad + 4, :].bitcast(I32)
+            )
+        nc.scalar.dma_start(out=out_rows[:, PACK - 1, :], in_=late[:])

@@ -56,8 +56,8 @@ def tile_attend_maxmerge_pl_kernel(tc, query, keys, size, vals, vsc, offs, offs2
         make_identity(nc, ident[:])
         nc.scalar.activation(out=warm[:, 1:2], in_=warm[:, 0:1], func=ACT.Exp)
 
-        nc.sync.dma_start(list_a[:], offs)
         nc.sync.dma_start(out=key_win[0][:], in_=key_planes[0])
+        nc.sync.dma_start(list_a[:], offs)
         nc.sync.dma_start(list_b[:], offs2)
         nc.sync.dma_start(out=key_win[1][:], in_=key_planes[1])
         nc.sync.dma_start(out=q_raw[:], in_=query.rearrange("(p t) q -> p t q", t=PACK))
@@ -81,7 +81,7 @@ def tile_attend_maxmerge_pl_kernel(tc, query, keys, size, vals, vsc, offs, offs2
 
         factor_bank = ps.tile([P, P], F32, name="factor_bank")
         nc.tensor.transpose(factor_bank[:], factor_rows[:], ident[:])
-        size_cols = sb.tile([P, PACK], F32, name="size_cols", tag="slot_2_1", align_bytes=64)
+        size_cols = sb.tile([P, PACK], F32, name="size_cols")
         vsc_cols = sb.tile([P, PACK], F32, name="vsc_cols")
         nc.scalar.copy(out=size_cols[:], in_=factor_bank[:, 0:PACK])
         nc.scalar.copy(out=vsc_cols[:], in_=factor_bank[:, PACK : 2 * PACK])
@@ -94,12 +94,19 @@ def tile_attend_maxmerge_pl_kernel(tc, query, keys, size, vals, vsc, offs, offs2
             if t == 2:
                 nc.vector.quantize_mx(out=q_codes[:].bitcast(FP8X4), scales=q_scales[:], in_=flat(q_bf[:]))
         km_bf = sb.tile([P, I, PACK], BF16, name="km_bf", align_bytes=64)
-        km_codes = sb.tile([P, I], U32, name="km_codes", align_bytes=64)
+        km_codes = sb.tile([P, I], U32, name="km_codes", tag="slot_1_0", align_bytes=64)
         km_scales = sb.tile([P, I], U8, name="km_scales", align_bytes=64)
         nc.vector.tensor_tensor(out=woven(km_bf[:]), in0=planar(key_a[:]), in1=planar(key_b[:]), op=ALU.max)
 
+        last_pair = {}
+
         def gather_vals(r, which):
-            got = sb.tile([P, I], F32, name="val_%d_%d" % (r, which), tag="slot_%d_%d" % (r, which), align_bytes=64)
+            if r < 2:
+                got = sb.tile([P, I], F32, name="val_%d_%d" % (r, which), tag="slot_%d_%d" % (r, which), align_bytes=64)
+            else:
+                if which == 0:
+                    last_pair[r] = sb.tile([P, 2 * I], F32, name="val_%d" % r, tag="slot_%d" % r, align_bytes=64)
+                got = last_pair[r][:, which * I : (which + 1) * I]
             nc.vector.tensor_copy(
                 got[:].bitcast(U32).rearrange("p (t b j) -> p b t j", t=PACK, j=8),
                 val_win[r][:].bitcast(U32).indirect((list_a, list_b)[which][:]),
@@ -116,15 +123,31 @@ def tile_attend_maxmerge_pl_kernel(tc, query, keys, size, vals, vsc, offs, offs2
         def spread(col):
             return col.unsqueeze(1).unsqueeze(3).to_broadcast([P, P // 2, PACK, 2])
 
-        vv_bf = [sb.tile([P, P, PACK], BF16, name="vv_bf%d" % r, tag=("slot_3_0", "slot_3_1", "vv_bf2", "vv_bf3")[r], align_bytes=64) for r in range(PACK)]
-        vv_codes = [sb.tile([P, P], U32, name="vv_codes%d" % r, align_bytes=64) for r in range(PACK)]
-        vv_scales = [sb.tile([P, P], U8, name="vv_scales%d" % r, align_bytes=64) for r in range(PACK)]
+        joint_bf = sb.tile([P, Q + 2 * P, PACK], BF16, name="joint_bf", align_bytes=64)
+        joint_codes = sb.tile([P, Q + 2 * P], U32, name="joint_codes", align_bytes=64)
+        joint_scales = sb.tile([P, Q + 2 * P], U8, name="joint_scales", align_bytes=64)
+        w_bf, w_codes, w_scales = joint_bf[:, 0:Q, :], joint_codes[:, 0:Q], joint_scales[:, 0:Q]
+        vv_bf = [joint_bf[:, Q + r * P : Q + (r + 1) * P, :] for r in range(2)]
+        vv_codes = [joint_codes[:, Q + r * P : Q + (r + 1) * P] for r in range(2)]
+        vv_scales = [joint_scales[:, Q + r * P : Q + (r + 1) * P] for r in range(2)]
+        for r in range(2, PACK):
+            vv_bf.append(sb.tile([P, P, PACK], BF16, name="vv_bf%d" % r, align_bytes=64))
+            vv_codes.append(sb.tile([P, P], U32, name="vv_codes%d" % r, align_bytes=64))
+            vv_scales.append(sb.tile([P, P], U8, name="vv_scales%d" % r, align_bytes=64))
         v_bank = {}
 
         def value_step(r, which):
             if which == 0:
-                v_bank[r] = ps.tile([P, PACK, P], F32, name="v_bank", tag="v_bank", bufs=3)
+                v_bank[r] = ps.tile([P, PACK, P], F32, name="v_bank", tag="v_bank", bufs=2)
             turn(v_bank[r], gather_vals(r, which), which == 0, which == 1)
+
+        def scale_on_scalar(out, bank, cols, label):
+            scaled = sb.tile([P, PACK, P], BF16, name="scaled_" + label)
+            for t in range(PACK):
+                nc.scalar.activation(out=scaled[:, t, :], in_=bank[:, t, :], func=ACT.Copy, scale=cols[:, t : t + 1])
+            nc.scalar.copy(
+                out=out.rearrange("p (c i) t -> p c t i", i=4), in_=scaled[:].rearrange("p t (c i) -> p c t i", i=4)
+            )
 
         def scale_vals(r):
             if r == PACK - 1:
@@ -132,10 +155,7 @@ def tile_attend_maxmerge_pl_kernel(tc, query, keys, size, vals, vsc, offs, offs2
                     out=woven(vv_bf[r][:]), in0=planar(v_bank[r][:]), in1=spread(vsc_cols[:]), op=ALU.mult
                 )
             else:
-                for t in range(PACK):
-                    nc.scalar.activation(
-                        out=vv_bf[r][:, :, t], in_=v_bank[r][:, t, :], func=ACT.Copy, scale=vsc_cols[:, t : t + 1]
-                    )
+                scale_on_scalar(vv_bf[r][:], v_bank[r], vsc_cols, "v%d" % r)
 
         def quantize_vals(r):
             nc.vector.quantize_mx(out=vv_codes[r][:].bitcast(FP8X4), scales=vv_scales[r][:], in_=flat(vv_bf[r][:]))
@@ -151,11 +171,11 @@ def tile_attend_maxmerge_pl_kernel(tc, query, keys, size, vals, vsc, offs, offs2
             )
         value_step(0, 1)
 
-        neg_max = [sb.tile([P, 1], F32, name="neg_max%d" % h, tag=("slot_1_0", "neg_max1")[h], align_bytes=64) for h in range(HALVES)]
-        sums = sb.tile([P, HALVES], F32, name="sums", tag="slot_1_1", align_bytes=64)
+        neg_max = [sb.tile([P, 1], F32, name="neg_max%d" % h, tag=("neg_max0", "slot_1_1")[h], align_bytes=64) for h in range(HALVES)]
+        sums = sb.tile([P, HALVES], F32, name="sums")
         inv = sb.tile([P, HALVES], F32, name="inv")
-        prob = [sb.tile([P, I], F32, name="prob%d" % h) for h in range(HALVES)]
-        normed = [sb.tile([P, I], F32, name="normed%d" % h) for h in range(HALVES)]
+        prob = [sb.tile([P, I], F32, name="prob%d" % h, tag=("slot_2", "prob1")[h], align_bytes=64) for h in range(HALVES)]
+        normed = [sb.tile([P, I], F32, name="normed%d" % h, tag=("normed0", "slot_3")[h], align_bytes=64) for h in range(HALVES)]
         for h in range(HALVES):
             nc.vector.tensor_reduce(out=neg_max[h][:], in_=scores[h][:], axis=mybir.AxisListType.X, op=ALU.max, negate=True)
             nc.scalar.activation(
@@ -174,62 +194,55 @@ def tile_attend_maxmerge_pl_kernel(tc, query, keys, size, vals, vsc, offs, offs2
         scale_vals(0)
         value_step(1, 1)
         value_step(2, 0)
-        w_bf = sb.tile([P, Q, PACK], BF16, name="w_bf", align_bytes=64)
-        w_codes = sb.tile([P, Q], U32, name="w_codes", align_bytes=64)
-        w_scales = sb.tile([P, Q], U8, name="w_scales", align_bytes=64)
-        for h in range(HALVES):
-            nc.vector.tensor_tensor(
-                out=woven(w_bf[:, h * P : (h + 1) * P, :]), in0=planar(w_bank[h][:]), in1=spread(size_cols[:]), op=ALU.mult
-            )
-        scale_vals(1)
         value_step(2, 1)
-        nc.vector.quantize_mx(out=w_codes[:].bitcast(FP8X4), scales=w_scales[:], in_=flat(w_bf[:]))
-        quantize_vals(0)
-        quantize_vals(1)
+        nc.vector.tensor_tensor(out=woven(w_bf[:, 0:P, :]), in0=planar(w_bank[0][:]), in1=spread(size_cols[:]), op=ALU.mult)
+        scale_vals(1)
+        scale_on_scalar(w_bf[:, P:Q, :], w_bank[1], size_cols, "w")
         scale_vals(2)
+        value_step(3, 0)
+        value_step(3, 1)
+        nc.vector.quantize_mx(out=joint_codes[:].bitcast(FP8X4), scales=joint_scales[:], in_=flat(joint_bf[:]))
 
         out_bank = [ps.tile([P, PACK, P], F32, name="out_bank%d" % h) for h in range(HALVES)]
 
-        def product(r):
-            for h in range(HALVES):
-                nc.tensor.matmul_mx(
-                    out=out_bank[h][:, r, :],
-                    lhsT=vv_codes[r][:].bitcast(FP8X4), lhsT_scale=vv_scales[r][:],
-                    rhs=w_codes[:, h * P : (h + 1) * P].bitcast(FP8X4), rhs_scale=w_scales[:, h * P : (h + 1) * P],
-                    start=True, stop=True,
-                )
+        def product(r, h):
+            nc.tensor.matmul_mx(
+                out=out_bank[h][:, r, :],
+                lhsT=vv_codes[r][:].bitcast(FP8X4), lhsT_scale=vv_scales[r][:],
+                rhs=w_codes[:, h * P : (h + 1) * P].bitcast(FP8X4), rhs_scale=w_scales[:, h * P : (h + 1) * P],
+                start=True, stop=True,
+            )
 
-        product(0)
-        product(1)
-        value_step(3, 0)
-        value_step(3, 1)
-        quantize_vals(2)
-        product(2)
         out_rows = out_0.rearrange("(p r) q -> p r q", r=PACK)
-        early = sb.tile([P, PACK - 1, Q], F32, name="early")
-        late = sb.tile([P, Q], F32, name="late")
+        early = sb.tile([P, 2, Q], F32, name="early")
+        late = [sb.tile([P, 2, P], F32, name="late%d" % h) for h in range(HALVES)]
         for h in range(HALVES):
-            nc.scalar.copy(out=early[:, :, h * P : (h + 1) * P], in_=out_bank[h][:, 0 : PACK - 1, :])
-        nc.sync.dma_start(out=out_rows[:, 0 : PACK - 1, :], in_=early[:])
+            product(0, h)
+            product(1, h)
+            nc.scalar.copy(out=early[:, :, h * P : (h + 1) * P], in_=out_bank[h][:, 0:2, :])
+        nc.sync.dma_start(out=out_rows[:, 0:2, :], in_=early[:])
         scale_vals(3)
+        quantize_vals(2)
         quantize_vals(3)
-        product(3)
+        for h in range(HALVES):
+            for r in range(2, PACK):
+                product(r, h)
 
-        o_bf = [sb.tile([P, P, PACK], BF16, name="o_bf%d" % h, align_bytes=64) for h in range(HALVES)]
+        o_bf = sb.tile([P, Q, PACK], BF16, name="o_bf", align_bytes=64)
         o_codes = sb.tile([P, Q], U32, name="o_codes", align_bytes=64)
         o_scales = sb.tile([P, Q], U8, name="o_scales", align_bytes=64)
-        nc.vector.tensor_copy(out=woven(o_bf[0][:]), in_=planar(out_bank[0][:]))
-        nc.scalar.copy(out=woven(o_bf[1][:]), in_=planar(out_bank[1][:]))
+        nc.vector.tensor_copy(out=woven(o_bf[:, 0:P, :]), in_=planar(out_bank[0][:]))
+        nc.scalar.copy(out=woven(o_bf[:, P:Q, :]), in_=planar(out_bank[1][:]))
+        nc.vector.tensor_copy(out=late[0][:], in_=out_bank[0][:, 2:4, :])
+        nc.scalar.copy(out=late[1][:], in_=out_bank[1][:, 2:4, :])
+        nc.sync.dma_start(out=out_rows[:, 2:4, 0:P], in_=late[0][:])
+        nc.scalar.dma_start(out=out_rows[:, 2:4, P:Q], in_=late[1][:])
         for h in range(HALVES):
-            nc.vector.quantize_mx(
-                out=o_codes[:, h * P : (h + 1) * P].bitcast(FP8X4), scales=o_scales[:, h * P : (h + 1) * P], in_=flat(o_bf[h][:])
-            )
-        for h in range(HALVES):
-            nc.scalar.copy(out=late[:, h * P : (h + 1) * P], in_=out_bank[h][:, PACK - 1, :])
+            cols = slice(h * P, (h + 1) * P)
+            nc.vector.quantize_mx(out=o_codes[:, cols].bitcast(FP8X4), scales=o_scales[:, cols], in_=flat(o_bf[:, cols, :]))
         nc.sync.dma_start(out=out_1[0].rearrange("p c r -> p (c r)").bitcast(I32), in_=o_codes[:].bitcast(I32))
         for quad in range(4):
             queue = nc.sync if quad % 2 == 0 else nc.scalar
             queue.dma_start(
                 out=out_2[0, 4 * quad : 4 * quad + 4, :].bitcast(I32), in_=o_scales[32 * quad : 32 * quad + 4, :].bitcast(I32)
             )
-        nc.scalar.dma_start(out=out_rows[:, PACK - 1, :], in_=late[:])

from contextlib import ExitStack

import concourse.mybir as mybir
from concourse.masks import make_identity

D, T, I, Q, E = 512, 1024, 512, 256, 512
FLOPS = 2 * D * Q * I + 2 * I * E * Q

F32 = mybir.dt.float32
BF16 = mybir.dt.bfloat16
U32 = mybir.dt.uint32
I32 = mybir.dt.int32
U16 = mybir.dt.uint16
U8 = mybir.dt.uint8
FP8X4 = mybir.dt.float8_e4m3fn_x4
ALU = mybir.AluOpType
ACT = mybir.ActivationFunctionType

P = 128
PACK = 4
HALVES = Q // P


def woven(ap):
    return ap.rearrange("p (c i) t -> p c t i", i=2)


def planar(ap):
    return ap.rearrange("p t (c i) -> p c t i", i=2)


def flat(ap):
    return ap.rearrange("p c t -> p (c t)")


def tile_attend_maxmerge_pl_kernel(tc, query, keys, size, vals, vsc, offs, offs2, out_0, out_1, out_2):
    nc = tc.nc
    with ExitStack() as ctx:
        lists = ctx.enter_context(tc.tile_pool(name="lists", bufs=1))
        sb = ctx.enter_context(tc.tile_pool(name="sb", bufs=1))
        ps = ctx.enter_context(tc.psum_pool(name="ps", bufs=1))

        list_a = lists.tile([P, I // 16], U16, name="list_a")
        list_b = lists.tile([P, I // 16], U16, name="list_b")
        key_planes = keys.rearrange("(p t) n -> t p n", t=PACK)
        val_planes = vals.rearrange("(p t) n -> t p n", t=PACK)
        key_win = [sb.tile([P, T], F32, name="key_win%d" % t) for t in range(PACK)]
        val_win = [sb.tile([P, T], F32, name="val_win%d" % t) for t in range(PACK)]
        q_raw = sb.tile([P, PACK, Q], F32, name="q_raw")
        factor_rows = sb.tile([P, P], F32, name="factor_rows")
        ident = sb.tile([P, P], F32, name="ident")
        warm = sb.tile([P, 2], F32, name="warm")

        nc.vector.memset(factor_rows[:], 0.0)
        nc.vector.memset(warm[:, 0:1], 0.0)
        make_identity(nc, ident[:])
        nc.scalar.activation(out=warm[:, 1:2], in_=warm[:, 0:1], func=ACT.Exp)

        nc.sync.dma_start(out=key_win[0][:], in_=key_planes[0])
        nc.sync.dma_start(list_a[:], offs)
        nc.sync.dma_start(list_b[:], offs2)
        nc.sync.dma_start(out=key_win[1][:], in_=key_planes[1])
        nc.sync.dma_start(out=q_raw[:], in_=query.rearrange("(p t) q -> p t q", t=PACK))
        nc.sync.dma_start(out=key_win[2][:], in_=key_planes[2])
        nc.sync.dma_start(out=key_win[3][:], in_=key_planes[3])
        nc.sync.dma_start(
            out=factor_rows[0:PACK, :].rearrange("t (b j) -> t b j", j=8),
            in_=size.rearrange("o (b t j) -> (o t) b j", t=PACK, j=8),
        )
        nc.sync.dma_start(
            out=factor_rows[PACK : 2 * PACK, :].rearrange("t (b j) -> t b j", j=8),
            in_=vsc.rearrange("(b t j) o -> t b (j o)", t=PACK, j=8),
        )
        for r in range(PACK):
            nc.sync.dma_start(out=val_win[r][:], in_=val_planes[r])

        q_bf = sb.tile([P, Q, PACK], BF16, name="q_bf", align_bytes=64)
        q_codes = sb.tile([P, Q], U32, name="q_codes", align_bytes=64)
        q_scales = sb.tile([P, Q], U8, name="q_scales", align_bytes=64)
        nc.scalar.copy(out=woven(q_bf[:]), in_=planar(q_raw[:]))

        factor_bank = ps.tile([P, P], F32, name="factor_bank")
        nc.tensor.transpose(factor_bank[:], factor_rows[:], ident[:])
        size_cols = sb.tile([P, PACK], F32, name="size_cols")
        vsc_cols = sb.tile([P, PACK], F32, name="vsc_cols")
        nc.scalar.copy(out=size_cols[:], in_=factor_bank[:, 0:PACK])
        nc.scalar.copy(out=vsc_cols[:], in_=factor_bank[:, PACK : 2 * PACK])

        key_a = sb.tile([P, PACK, I], F32, name="key_a")
        key_b = sb.tile([P, PACK, I], F32, name="key_b")
        for t in range(PACK):
            nc.vector.tensor_copy(key_a[:, t, :], key_win[t][:].indirect(list_a[:]))
            nc.vector.tensor_copy(key_b[:, t, :], key_win[t][:].indirect(list_b[:]))
            if t == 2:
                nc.vector.quantize_mx(out=q_codes[:].bitcast(FP8X4), scales=q_scales[:], in_=flat(q_bf[:]))
        km_bf = sb.tile([P, I, PACK], BF16, name="km_bf", align_bytes=64)
        km_codes = sb.tile([P, I], U32, name="km_codes", tag="slot_1_0", align_bytes=64)
        km_scales = sb.tile([P, I], U8, name="km_scales", align_bytes=64)
        nc.vector.tensor_tensor(out=woven(km_bf[:]), in0=planar(key_a[:]), in1=planar(key_b[:]), op=ALU.max)

        last_pair = {}

        def gather_vals(r, which):
            if r < 2:
                got = sb.tile([P, I], F32, name="val_%d_%d" % (r, which), tag="slot_%d_%d" % (r, which), align_bytes=64)
            else:
                if which == 0:
                    last_pair[r] = sb.tile([P, 2 * I], F32, name="val_%d" % r, tag="slot_%d" % r, align_bytes=64)
                got = last_pair[r][:, which * I : (which + 1) * I]
            nc.vector.tensor_copy(
                got[:].bitcast(U32).rearrange("p (t b j) -> p b t j", t=PACK, j=8),
                val_win[r][:].bitcast(U32).indirect((list_a, list_b)[which][:]),
            )
            return got

        def turn(bank, got, first, last):
            for t in range(PACK):
                nc.tensor.matmul(
                    out=bank[:, t, :], lhsT=got[:, t * P : (t + 1) * P], rhs=ident[:], is_transpose=True,
                    start=(first and t == 0), stop=(last and t == PACK - 1),
                )

        def spread(col):
            return col.unsqueeze(1).unsqueeze(3).to_broadcast([P, P // 2, PACK, 2])

        joint_bf = sb.tile([P, Q + 2 * P, PACK], BF16, name="joint_bf", align_bytes=64)
        joint_codes = sb.tile([P, Q + 2 * P], U32, name="joint_codes", align_bytes=64)
        joint_scales = sb.tile([P, Q + 2 * P], U8, name="joint_scales", align_bytes=64)
        w_bf, w_codes, w_scales = joint_bf[:, 0:Q, :], joint_codes[:, 0:Q], joint_scales[:, 0:Q]
        vv_bf = [joint_bf[:, Q + r * P : Q + (r + 1) * P, :] for r in range(2)]
        vv_codes = [joint_codes[:, Q + r * P : Q + (r + 1) * P] for r in range(2)]
        vv_scales = [joint_scales[:, Q + r * P : Q + (r + 1) * P] for r in range(2)]
        for r in range(2, PACK):
            vv_bf.append(sb.tile([P, P, PACK], BF16, name="vv_bf%d" % r, align_bytes=64))
            vv_codes.append(sb.tile([P, P], U32, name="vv_codes%d" % r, align_bytes=64))
            vv_scales.append(sb.tile([P, P], U8, name="vv_scales%d" % r, align_bytes=64))
        v_bank = {}

        def value_step(r, which):
            if which == 0:
                v_bank[r] = ps.tile([P, PACK, P], F32, name="v_bank", tag="v_bank", bufs=2)
            turn(v_bank[r], gather_vals(r, which), which == 0, which == 1)

        def scale_on_scalar(out, bank, cols, label):
            scaled = sb.tile([P, PACK, P], BF16, name="scaled_" + label)
            for t in range(PACK):
                nc.scalar.activation(out=scaled[:, t, :], in_=bank[:, t, :], func=ACT.Copy, scale=cols[:, t : t + 1])
            nc.scalar.copy(
                out=out.rearrange("p (c i) t -> p c t i", i=4), in_=scaled[:].rearrange("p t (c i) -> p c t i", i=4)
            )

        def scale_vals(r):
            if r == PACK - 1:
                nc.vector.tensor_tensor(
                    out=woven(vv_bf[r][:]), in0=planar(v_bank[r][:]), in1=spread(vsc_cols[:]), op=ALU.mult
                )
            else:
                scale_on_scalar(vv_bf[r][:], v_bank[r], vsc_cols, "v%d" % r)

        def quantize_vals(r):
            nc.vector.quantize_mx(out=vv_codes[r][:].bitcast(FP8X4), scales=vv_scales[r][:], in_=flat(vv_bf[r][:]))

        value_step(0, 0)
        nc.vector.quantize_mx(out=km_codes[:].bitcast(FP8X4), scales=km_scales[:], in_=flat(km_bf[:]))
        scores = [ps.tile([P, I], F32, name="scores", tag="scores", bufs=2) for h in range(HALVES)]
        for h in range(HALVES):
            nc.tensor.matmul_mx(
                out=scores[h][:],
                lhsT=q_codes[:, h * P : (h + 1) * P].bitcast(FP8X4), lhsT_scale=q_scales[:, h * P : (h + 1) * P],
                rhs=km_codes[:].bitcast(FP8X4), rhs_scale=km_scales[:], start=True, stop=True,
            )
        value_step(0, 1)

        neg_max = [sb.tile([P, 1], F32, name="neg_max%d" % h, tag=("neg_max0", "slot_1_1")[h], align_bytes=64) for h in range(HALVES)]
        sums = sb.tile([P, HALVES], F32, name="sums")
        inv = sb.tile([P, HALVES], F32, name="inv")
        prob = [sb.tile([P, I], F32, name="prob%d" % h, tag=("slot_2", "prob1")[h], align_bytes=64) for h in range(HALVES)]
        normed = [sb.tile([P, I], F32, name="normed%d" % h, tag=("normed0", "slot_3")[h], align_bytes=64) for h in range(HALVES)]
        for h in range(HALVES):
            nc.vector.tensor_reduce(out=neg_max[h][:], in_=scores[h][:], axis=mybir.AxisListType.X, op=ALU.max, negate=True)
            nc.scalar.activation(
                out=prob[h][:].rearrange("p (t b j) -> p t b j", t=PACK, j=8),
                in_=scores[h][:].rearrange("p (b t j) -> p t b j", t=PACK, j=8),
                func=ACT.Exp, bias=neg_max[h][:], accum_out=sums[:, h : h + 1],
            )
        value_step(1, 0)
        nc.vector.reciprocal(out=inv[:], in_=sums[:])
        w_bank = []
        for h in range(HALVES):
            nc.scalar.activation(out=normed[h][:], in_=prob[h][:], func=ACT.Copy, scale=inv[:, h : h + 1])
            bank = ps.tile([P, PACK, P], F32, name="w_bank", tag="scores", bufs=2)
            turn(bank, normed[h], True, True)
            w_bank.append(bank)
        scale_vals(0)
        value_step(1, 1)
        value_step(2, 0)
        value_step(2, 1)
        nc.vector.tensor_tensor(out=woven(w_bf[:, 0:P, :]), in0=planar(w_bank[0][:]), in1=spread(size_cols[:]), op=ALU.mult)
        scale_vals(1)
        scale_on_scalar(w_bf[:, P:Q, :], w_bank[1], size_cols, "w")
        scale_vals(2)
        value_step(3, 0)
        value_step(3, 1)
        nc.vector.quantize_mx(out=joint_codes[:].bitcast(FP8X4), scales=joint_scales[:], in_=flat(joint_bf[:]))

        out_bank = [ps.tile([P, PACK, P], F32, name="out_bank%d" % h) for h in range(HALVES)]

        def product(r, h):
            nc.tensor.matmul_mx(
                out=out_bank[h][:, r, :],
                lhsT=vv_codes[r][:].bitcast(FP8X4), lhsT_scale=vv_scales[r][:],
                rhs=w_codes[:, h * P : (h + 1) * P].bitcast(FP8X4), rhs_scale=w_scales[:, h * P : (h + 1) * P],
                start=True, stop=True,
            )

        out_rows = out_0.rearrange("(p r) q -> p r q", r=PACK)
        early = sb.tile([P, 2, Q], F32, name="early")
        late = [sb.tile([P, 2, P], F32, name="late%d" % h) for h in range(HALVES)]
        for h in range(HALVES):
            product(0, h)
            product(1, h)
            nc.scalar.copy(out=early[:, :, h * P : (h + 1) * P], in_=out_bank[h][:, 0:2, :])
        nc.sync.dma_start(out=out_rows[:, 0:2, :], in_=early[:])
        scale_vals(3)
        quantize_vals(2)
        quantize_vals(3)
        for h in range(HALVES):
            for r in range(2, PACK):
                product(r, h)

        o_bf = sb.tile([P, Q, PACK], BF16, name="o_bf", align_bytes=64)
        o_codes = sb.tile([P, Q], U32, name="o_codes", align_bytes=64)
        o_scales = sb.tile([P, Q], U8, name="o_scales", align_bytes=64)
        nc.vector.tensor_copy(out=woven(o_bf[:, 0:P, :]), in_=planar(out_bank[0][:]))
        nc.scalar.copy(out=woven(o_bf[:, P:Q, :]), in_=planar(out_bank[1][:]))
        nc.vector.tensor_copy(out=late[0][:], in_=out_bank[0][:, 2:4, :])
        nc.scalar.copy(out=late[1][:], in_=out_bank[1][:, 2:4, :])
        nc.sync.dma_start(out=out_rows[:, 2:4, 0:P], in_=late[0][:])
        nc.scalar.dma_start(out=out_rows[:, 2:4, P:Q], in_=late[1][:])
        for h in range(HALVES):
            cols = slice(h * P, (h + 1) * P)
            nc.vector.quantize_mx(out=o_codes[:, cols].bitcast(FP8X4), scales=o_scales[:, cols], in_=flat(o_bf[:, cols, :]))
        nc.sync.dma_start(out=out_1[0].rearrange("p c r -> p (c r)").bitcast(I32), in_=o_codes[:].bitcast(I32))
        for quad in range(4):
            queue = nc.sync if quad % 2 == 0 else nc.scalar
            queue.dma_start(
                out=out_2[0, 4 * quad : 4 * quad + 4, :].bitcast(I32), in_=o_scales[32 * quad : 32 * quad + 4, :].bitcast(I32)
            )
